import numpy as np
import ml_dtypes


def mxq(x, axis, fmt="e4m3"):
    dtype, down = {"e4m3": (ml_dtypes.float8_e4m3fn, 7), "e5m2": (ml_dtypes.float8_e5m2, 14)}[fmt]
    v = np.moveaxis(np.asarray(x, np.float32).astype(ml_dtypes.bfloat16).astype(np.float64), axis, -1)
    blocks = v.reshape(v.shape[:-1] + (-1, 32))
    amax = np.abs(blocks).max(-1, keepdims=True)
    byte = np.maximum(np.where(amax > 0, np.frexp(amax)[1] - 1 + 127, 0) - down, 1)
    scale = np.exp2(byte - 127.0)
    codes = (blocks / scale).astype(np.float32).astype(dtype).astype(np.float64)
    return np.moveaxis((codes * scale).reshape(v.shape), -1, axis)


WIDE = False


def mx_kscale(k):
    if not WIDE:
        return np.ones(k)
    levels = np.array([10, -10, 5, -5, 0])
    if k % 512:
        return np.exp2(np.random.permutation(np.resize(levels, k // 32))).repeat(32)
    a = np.empty((k // 512, 16))
    for p in range(k // 512):
        a[p, :8] = np.random.permutation(np.resize(levels, 8))
        for g in range(8):
            far = levels[np.abs(levels - a[p, g]) >= 10]
            a[p, g + 8] = far[np.random.randint(len(far))]
    return np.exp2(a.ravel()).repeat(32)


def f64(x):
    return np.asarray(x).astype(np.float64)


def striped(idx):
    return np.tile(idx.reshape(-1, 16).T, (8, 1)).astype(np.uint16)


def unstriped(offs):
    return offs[:16].T.reshape(-1).astype(np.int64)


def striped8(idx):
    return np.concatenate([x.reshape(-1, 16).T for x in idx]).astype(np.uint16)


def runs(offs, k):
    lists = np.stack([offs[16 * r : 16 * r + 16].T.reshape(-1) for r in range(8)]).astype(np.int64)
    return lists[np.arange(k) % 512 // 64]


def pack_weight(w):
    k, n = w.shape
    w = f64(np.asarray(w, np.float32).astype(ml_dtypes.bfloat16)).reshape(k // 32, 32, n)
    amax = np.abs(w).max(1)
    byte = np.clip(np.where(amax > 0, np.frexp(amax)[1] - 1 + 127 - 7, 1), 1, 254)
    scaled = (w * np.exp2(127.0 - byte)[:, None, :]).reshape(k, n).astype(np.float32)
    words = np.ascontiguousarray(scaled.reshape(k // 512, 128, 4, n).transpose(0, 1, 3, 2)).astype(ml_dtypes.float8_e4m3fn).view(np.uint8)
    return words, np.ascontiguousarray(byte.astype(np.uint8).reshape(k // 512, 16, n))


def unpack_weight(words, scales):
    g, p, n, _ = words.shape
    vals = np.ascontiguousarray(words).view(ml_dtypes.float8_e4m3fn).astype(np.float64) * np.repeat(np.exp2(scales.astype(np.float64) - 127.0), 8, axis=1)[..., None]
    return vals.transpose(0, 1, 3, 2).reshape(g * 512, n)


K, T, S, N, H, W = 512, 2048, 512, 512, 512, 256


def setup_inputs():
    n = np.random.standard_normal
    s = mx_kscale(K)[:, None]
    u = mx_kscale(S)
    packed_xT = pack_weight(n((K, T)) * s)
    perm = np.stack([np.random.permutation(H) for _ in range(8)])
    return {
        "x_words": packed_xT[0],
        "x_scales": packed_xT[1],
        "wa": (n((K, H)) / np.sqrt(K) / s).astype(np.float32),
        "gt": (np.random.uniform(0.5, 1.5, (S, 1)) * u[:, None]).astype(np.float32),
        "w1": (n((S, N)) / np.sqrt(S) / u[:, None]).astype(np.float32),
        "offs": striped(np.random.permutation(T)[:S]),
        "n1": striped8(perm[:, :W]),
        "n2": striped8(perm[:, W:]),
        "n3": striped8(np.stack([np.random.permutation(H) for _ in range(8)])),
        "n4": striped8(np.stack([np.random.permutation(H) for _ in range(8)])),
    }


def reference(x_words, x_scales, wa, gt, w1, offs, n1, n2, n3, n4):
    xq = unpack_weight(x_words, x_scales)[:, unstriped(offs)]
    y = xq.T @ mxq(f64(wa), 0, "e4m3")
    pa = y[np.arange(S)[:, None], runs(n1, S)]
    pb = y[np.arange(S)[:, None], runs(n2, S)]
    ra = np.maximum(pa, pb)
    ds = y.copy()
    ds[np.arange(S)[:, None], runs(n1, S)] = ra
    z = f64(gt) * ds
    h = mxq(f64(w1), 0, "e4m3").T @ mxq(z, 0, "e4m3")
    st = h + h[np.arange(N)[:, None], runs(n3, N)]
    return st * (np.tanh(st[np.arange(N)[:, None], runs(n4, N)]))

@@ -1,0 +1,179 @@
+from contextlib import ExitStack
+
+import concourse.mybir as mybir
+
+K, T, S, N, H, W = 512, 2048, 512, 512, 512, 256
+FLOPS = 2 * K * S * H + 2 * S * N * H
+
+F32 = mybir.dt.float32
+BF16 = mybir.dt.bfloat16
+I32 = mybir.dt.int32
+U32 = mybir.dt.uint32
+U16 = mybir.dt.uint16
+U8 = mybir.dt.uint8
+FP8X4 = mybir.dt.float8_e4m3fn_x4
+ALU = mybir.AluOpType
+ACT = mybir.ActivationFunctionType
+
+P = 128
+PACK = 4
+HALF = H // 2
+HALVES = (slice(0, HALF), slice(HALF, H))
+LIST_HALVES = (slice(0, HALF // 16), slice(HALF // 16, H // 16))
+
+
+def tile_picked_tokfillhopp_none_p_kernel(tc, x_words, x_scales, wa, gt, w1, offs, n1, n2, n3, n4, out):
+    nc = tc.nc
+    with ExitStack() as ctx:
+        keep = ctx.enter_context(tc.tile_pool(name="keep", bufs=1))
+        psum = ctx.enter_context(tc.psum_pool(name="psum", bufs=1))
+
+        def sb(name, shape, dtype, tag=None):
+            return keep.tile(shape, dtype, name=name, tag=tag or name, align_bytes=64)
+
+        def bank(name, number, width):
+            return psum.tile([P, width], F32, name=name, tag="bank%d" % number)
+
+        def load_list(name, src):
+            t = sb(name, list(src.shape), U16)
+            nc.sync.dma_start(t[:], src)
+            return t
+
+        all_scales = sb("all_scales", [P, T], U8)
+        nc.vector.memset(all_scales[:].bitcast(I32), 0)
+        for q in range(4):
+            nc.scalar.dma_start(all_scales[32 * q : 32 * q + 4, :].bitcast(I32), x_scales[0, 4 * q : 4 * q + 4, :].bitcast(I32))
+        zero = sb("zero", [P, 1], F32)
+        nc.vector.memset(zero[:], 0.0)
+        midpoint = sb("midpoint", [P, 1], F32)
+        nc.scalar.activation(midpoint[:], zero[:], ACT.Sigmoid)
+
+        offs_sb = load_list("offs_sb", offs)
+        all_words = sb("all_words", [P, T], I32)
+        nc.sync.dma_start(all_words[:], x_words[0].rearrange("p n r -> p (n r)").bitcast(I32))
+        wa_rows = wa.rearrange("(p j) c -> p j c", j=PACK)
+        wa_raw = [sb("wa_raw%d" % u, [P, PACK, HALF], F32) for u in range(2)]
+        for u in range(2):
+            nc.sync.dma_start(wa_raw[u][:], wa_rows[:, :, HALVES[u]])
+        n1_sb = load_list("n1_sb", n1)
+        n2_sb = load_list("n2_sb", n2)
+        w1_raw = sb("w1_raw", [P, PACK, N], F32)
+        nc.sync.dma_start(w1_raw[:], w1.rearrange("(p j) m -> p j m", j=PACK))
+        gt_sb = sb("gt_sb", [P, PACK], F32)
+        nc.sync.dma_start(gt_sb[:], gt.rearrange("(p t) o -> p (t o)", t=PACK))
+        n3_sb = load_list("n3_sb", n3)
+        n4_sb = load_list("n4_sb", n4)
+
+        picked_scales = sb("picked_scales", [P, S], U8)
+        nc.vector.tensor_copy(picked_scales[:], all_scales[:].indirect(offs_sb[:]))
+        x_sc = sb("x_sc", [P, S], U8)
+        nc.vector.tensor_copy(x_sc[:].rearrange("p (t m) -> p m t", t=PACK), picked_scales[:].rearrange("p (m t) -> p m t", t=PACK))
+        x_codes = sb("x_codes", [P, S], U32)
+        nc.vector.tensor_copy(x_codes[:].rearrange("p (t m) -> p m t", t=PACK), all_words[:].bitcast(U32).indirect(offs_sb[:]))
+
+        wa_codes = sb("wa_codes", [P, H], U32)
+        wa_sc = sb("wa_sc", [P, H], U8)
+        wa_bf = [sb("wa_bf%d" % u, [P, HALF, PACK], BF16) for u in range(2)]
+
+        def cast_wa(copy, u, cols):
+            copy(wa_bf[u][:, cols, :].rearrange("p (c i) j -> p c j i", i=4), wa_raw[u][:, :, cols].rearrange("p j (c i) -> p c j i", i=4))
+
+        def quantize(codes, scales, src):
+            nc.vector.quantize_mx(out=codes.bitcast(FP8X4), scales=scales, in_=src)
+
+        def product(dst, l_codes, l_sc, t, r_codes, r_sc, cols):
+            rows = slice(P * t, P * (t + 1))
+            nc.tensor.matmul_mx(out=dst, lhsT=l_codes[:, rows].bitcast(FP8X4), lhsT_scale=l_sc[:, rows], rhs=r_codes[:, cols].bitcast(FP8X4), rhs_scale=r_sc[:, cols], start=True, stop=True)
+
+        cast_wa(nc.vector.tensor_copy, 0, slice(0, HALF))
+        cast_wa(nc.vector.tensor_copy, 1, slice(0, 160))
+        cast_wa(nc.scalar.copy, 1, slice(160, HALF))
+        for u in range(2):
+            quantize(wa_codes[:, HALVES[u]], wa_sc[:, HALVES[u]], wa_bf[u][:].rearrange("p c j -> p (c j)"))
+
+        y = [sb("y%d" % t, [P, H], F32) for t in range(PACK)]
+        for u in range(2):
+            acc = bank("y0_%d" % u, u, HALF)
+            product(acc[:], x_codes, x_sc, 0, wa_codes, wa_sc, HALVES[u])
+            nc.scalar.copy(y[0][:, HALVES[u]], acc[:])
+        for t in range(1, PACK):
+            acc = bank("y%d_acc" % t, t + 1, H)
+            product(acc[:], x_codes, x_sc, t, wa_codes, wa_sc, slice(0, H))
+            nc.scalar.copy(y[t][:], acc[:])
+
+        w1_bf = sb("w1_bf", [P, N * PACK], BF16)
+        nc.scalar.copy(w1_bf[:].rearrange("p (t m j) -> p m j t", t=PACK, j=PACK), w1_raw[:].rearrange("p j (m t) -> p m j t", t=PACK))
+
+        pa = [sb("pa%d" % t, [P, W], F32) for t in range(PACK)]
+        gap = [sb("gap%d" % t, [P, W], F32) for t in range(PACK)]
+        rise = [sb("rise%d" % t, [P, W], F32) for t in range(PACK)]
+        for pair in ((0, 1), (2, 3)):
+            for t in pair:
+                nc.vector.tensor_copy(pa[t][:], y[t][:].indirect(n1_sb[:]))
+            for t in pair:
+                nc.vector.tensor_tensor(gap[t][:], y[t][:].indirect(n2_sb[:]), pa[t][:], ALU.subtract)
+        for t in range(PACK):
+            nc.scalar.activation(rise[t][:], gap[t][:], ACT.Relu)
+        z_bf = [sb("z_bf%d" % u, [P, HALF, PACK], BF16) for u in range(2)]
+        for t in range(PACK):
+            nc.vector.tensor_tensor(y[t][:].indirect(n1_sb[:]), pa[t][:], rise[t][:], ALU.add)
+            for u in range(2):
+                if t == PACK - 1 and u == 0:
+                    nc.vector.tensor_scalar(z_bf[u][:, :, t], y[t][:, HALVES[u]], gt_sb[:, t : t + 1], None, ALU.mult)
+                elif t == PACK - 2 and u == 0:
+                    nc.scalar.activation(z_bf[u][:, :, t : t + 2], y[t][:].rearrange("p (u c) -> p c u", u=2), ACT.Copy, scale=gt_sb[:, t : t + 1])
+                else:
+                    nc.scalar.activation(z_bf[u][:, :, t], y[t][:, HALVES[u]], ACT.Copy, scale=gt_sb[:, t : t + 1])
+
+        w1_codes = sb("w1_codes", [P, N], U32, tag="rise3")
+        w1_sc = sb("w1_sc", [P, N], U8)
+        z_codes = sb("z_codes", [P, H], U32)
+        z_sc = sb("z_sc", [P, H], U8)
+
+        def quantize_w1(cols):
+            quantize(w1_codes[:, cols], w1_sc[:, cols], w1_bf[:, PACK * cols.start : PACK * cols.stop])
+
+        quantize_w1(slice(0, P))
+        for u in range(2):
+            quantize(z_codes[:, HALVES[u]], z_sc[:, HALVES[u]], z_bf[u][:].rearrange("p c j -> p (c j)"))
+        quantize_w1(slice(P, 2 * P))
+        quantize_w1(slice(2 * P, 4 * P))
+
+        h2 = [sb("h2_%d" % t, [P, H], F32) for t in range(PACK)]
+        other = [sb("other%d" % t, [P, H], F32) for t in range(PACK)]
+        st2 = [sb("st2_%d" % t, [P, H], F32) for t in range(PACK)]
+        accs = []
+        for t in range(PACK):
+            if t == 0:
+                halves = [bank("h0_%d" % u, 5 + u, HALF)[:] for u in range(2)]
+                for u in range(2):
+                    product(halves[u], w1_codes, w1_sc, t, z_codes, z_sc, HALVES[u])
+                    nc.scalar.mul(h2[t][:, HALVES[u]], halves[u], 2.0)
+            else:
+                acc = bank("h%d_acc" % t, (6 + t) % 8, H)
+                halves = [acc[:, HALVES[u]] for u in range(2)]
+                product(acc[:], w1_codes, w1_sc, t, z_codes, z_sc, slice(0, H))
+                nc.scalar.mul(h2[t][:], acc[:], 2.0)
+                if t in (1, 2):
+                    nc.scalar.mul(other[t][:], acc[:], 2.0)
+            accs.append(halves)
+        for t in range(PACK):
+            if t in (1, 2):
+                for u in range(2):
+                    nc.vector.tensor_tensor(st2[t][:, HALVES[u]], h2[t][:].indirect(n3_sb[:, LIST_HALVES[u]]), other[t][:, HALVES[u]], ALU.add)
+            else:
+                for u in range(2):
+                    nc.vector.tensor_copy(other[t][:, HALVES[u]], h2[t][:].indirect(n3_sb[:, LIST_HALVES[u]]))
+                for u in range(2):
+                    nc.vector.scalar_tensor_tensor(st2[t][:, HALVES[u]], accs[t][u], 2.0, other[t][:, HALVES[u]], ALU.mult, ALU.add)
+
+        out_rows = out.rearrange("(p t) c -> p t c", t=PACK)
+        for t in range(PACK):
+            sig = sb("sig%d" % t, [P, H], F32)
+            res = sb("res%d" % t, [P, H], F32)
+            for u in range(2):
+                nc.scalar.activation(sig[:, HALVES[u]], st2[t][:].indirect(n4_sb[:, LIST_HALVES[u]]), ACT.Sigmoid)
+            pieces = HALVES if t == PACK - 1 else (slice(0, H),)
+            for cols in pieces:
+                nc.vector.scalar_tensor_tensor(res[:, cols], sig[:, cols], midpoint[:], st2[t][:, cols], ALU.subtract, ALU.mult)
+                nc.sync.dma_start(out_rows[:, t, cols], res[:, cols])

@@ -49,27 +49,16 @@ def tile_picked_tokfillhopp_none_p_kernel(tc, x_words, x_scales, wa, gt, w1, off
         nc.scalar.activation(midpoint[:], zero[:], ACT.Sigmoid)
 
         offs_sb = load_list("offs_sb", offs)
-        all_words = sb("all_words", [P, T], I32)
-        nc.sync.dma_start(all_words[:], x_words[0].rearrange("p n r -> p (n r)").bitcast(I32))
+        n1_sb = load_list("n1_sb", n1)
+        n2_sb = load_list("n2_sb", n2)
+        n3_sb = load_list("n3_sb", n3)
         wa_rows = wa.rearrange("(p j) c -> p j c", j=PACK)
         wa_raw = [sb("wa_raw%d" % u, [P, PACK, HALF], F32) for u in range(2)]
         for u in range(2):
             nc.sync.dma_start(wa_raw[u][:], wa_rows[:, :, HALVES[u]])
-        n1_sb = load_list("n1_sb", n1)
-        n2_sb = load_list("n2_sb", n2)
-        w1_raw = sb("w1_raw", [P, PACK, N], F32)
-        nc.sync.dma_start(w1_raw[:], w1.rearrange("(p j) m -> p j m", j=PACK))
-        gt_sb = sb("gt_sb", [P, PACK], F32)
-        nc.sync.dma_start(gt_sb[:], gt.rearrange("(p t) o -> p (t o)", t=PACK))
-        n3_sb = load_list("n3_sb", n3)
+        all_words = sb("all_words", [P, T], I32)
+        nc.sync.dma_start(all_words[:], x_words[0].rearrange("p n r -> p (n r)").bitcast(I32))
         n4_sb = load_list("n4_sb", n4)
-
-        picked_scales = sb("picked_scales", [P, S], U8)
-        nc.vector.tensor_copy(picked_scales[:], all_scales[:].indirect(offs_sb[:]))
-        x_sc = sb("x_sc", [P, S], U8)
-        nc.vector.tensor_copy(x_sc[:].rearrange("p (t m) -> p m t", t=PACK), picked_scales[:].rearrange("p (m t) -> p m t", t=PACK))
-        x_codes = sb("x_codes", [P, S], U32)
-        nc.vector.tensor_copy(x_codes[:].rearrange("p (t m) -> p m t", t=PACK), all_words[:].bitcast(U32).indirect(offs_sb[:]))
 
         wa_codes = sb("wa_codes", [P, H], U32)
         wa_sc = sb("wa_sc", [P, H], U8)
@@ -85,11 +74,28 @@ def tile_picked_tokfillhopp_none_p_kernel(tc, x_words, x_scales, wa, gt, w1, off
             rows = slice(P * t, P * (t + 1))
             nc.tensor.matmul_mx(out=dst, lhsT=l_codes[:, rows].bitcast(FP8X4), lhsT_scale=l_sc[:, rows], rhs=r_codes[:, cols].bitcast(FP8X4), rhs_scale=r_sc[:, cols], start=True, stop=True)
 
-        cast_wa(nc.vector.tensor_copy, 0, slice(0, HALF))
-        cast_wa(nc.vector.tensor_copy, 1, slice(0, 160))
-        cast_wa(nc.scalar.copy, 1, slice(160, HALF))
         for u in range(2):
+            if u == 0:
+                cast_wa(nc.vector.tensor_copy, u, slice(0, HALF))
+            else:
+                cast_wa(nc.vector.tensor_copy, u, slice(0, 160))
+                cast_wa(nc.scalar.copy, u, slice(160, HALF))
             quantize(wa_codes[:, HALVES[u]], wa_sc[:, HALVES[u]], wa_bf[u][:].rearrange("p c j -> p (c j)"))
+
+        w1_raw = sb("w1_raw", [P, PACK, N], F32, tag="wa_raw0")
+        gt_sb = sb("gt_sb", [P, PACK], F32, tag="wa_raw1")
+        for e in range(4):
+            nc.sync.dma_start(w1_raw[e:P:4, :, :], w1.rearrange("(a t e) m -> e a t m", t=PACK, e=4)[e])
+        with nc.allow_non_contiguous_dma(reason="gate weights, one value a token"):
+            for e in range(4):
+                nc.sync.dma_start(gt_sb[e:P:4, :], gt[:, 0].rearrange("(a t e) -> e a t", t=PACK, e=4)[e])
+
+        picked_scales = sb("picked_scales", [P, S], U8)
+        nc.vector.tensor_copy(picked_scales[:], all_scales[:].indirect(offs_sb[:]))
+        x_sc = sb("x_sc", [P, S], U8)
+        nc.vector.tensor_copy(x_sc[:].bitcast(I32).rearrange("p (t a) -> p a t", t=PACK), picked_scales[:].bitcast(I32).rearrange("p (a t) -> p a t", t=PACK))
+        x_codes = sb("x_codes", [P, S], U32, tag="picked_scales")
+        nc.vector.tensor_copy(x_codes[:].rearrange("p (t a e) -> p a t e", t=PACK, e=4), all_words[:].bitcast(U32).indirect(offs_sb[:]))
 
         y = [sb("y%d" % t, [P, H], F32) for t in range(PACK)]
         for u in range(2):
@@ -101,19 +107,23 @@ def tile_picked_tokfillhopp_none_p_kernel(tc, x_words, x_scales, wa, gt, w1, off
             product(acc[:], x_codes, x_sc, t, wa_codes, wa_sc, slice(0, H))
             nc.scalar.copy(y[t][:], acc[:])
 
-        w1_bf = sb("w1_bf", [P, N * PACK], BF16)
-        nc.scalar.copy(w1_bf[:].rearrange("p (t m j) -> p m j t", t=PACK, j=PACK), w1_raw[:].rearrange("p j (m t) -> p m j t", t=PACK))
-
         pa = [sb("pa%d" % t, [P, W], F32) for t in range(PACK)]
-        gap = [sb("gap%d" % t, [P, W], F32) for t in range(PACK)]
+        gap = sb("gap", [P, PACK * W], F32, tag="wa_codes")
         rise = [sb("rise%d" % t, [P, W], F32) for t in range(PACK)]
-        for pair in ((0, 1), (2, 3)):
-            for t in pair:
-                nc.vector.tensor_copy(pa[t][:], y[t][:].indirect(n1_sb[:]))
-            for t in pair:
-                nc.vector.tensor_tensor(gap[t][:], y[t][:].indirect(n2_sb[:]), pa[t][:], ALU.subtract)
         for t in range(PACK):
-            nc.scalar.activation(rise[t][:], gap[t][:], ACT.Relu)
+            nc.vector.tensor_copy(pa[t][:], y[t][:].indirect(n1_sb[:]))
+        for t in range(PACK):
+            nc.vector.tensor_tensor(gap[:, W * t : W * (t + 1)], y[t][:].indirect(n2_sb[:]), pa[t][:], ALU.subtract)
+
+        w1_bf = sb("w1_bf", [P, N * PACK], BF16, tag="picked_scales")
+
+        def cast_w1(ms):
+            nc.scalar.copy(w1_bf[:].rearrange("p (t m j) -> p m t j", t=PACK, j=PACK)[:, ms], w1_raw[:].rearrange("p j (m t) -> p m t j", t=PACK)[:, ms])
+
+        for ms, tiles in ((slice(0, 96), (0, 1)), (slice(96, P), (2, 3))):
+            cast_w1(ms)
+            for t in tiles:
+                nc.scalar.activation(rise[t][:], gap[:, W * t : W * (t + 1)], ACT.Relu)
         z_bf = [sb("z_bf%d" % u, [P, HALF, PACK], BF16) for u in range(2)]
         for t in range(PACK):
             nc.vector.tensor_tensor(y[t][:].indirect(n1_sb[:]), pa[t][:], rise[t][:], ALU.add)
@@ -125,19 +135,16 @@ def tile_picked_tokfillhopp_none_p_kernel(tc, x_words, x_scales, wa, gt, w1, off
                 else:
                     nc.scalar.activation(z_bf[u][:, :, t], y[t][:, HALVES[u]], ACT.Copy, scale=gt_sb[:, t : t + 1])
 
-        w1_codes = sb("w1_codes", [P, N], U32, tag="rise3")
-        w1_sc = sb("w1_sc", [P, N], U8)
+        w1_codes = [sb("w1_codes0", [P, P], U32, tag="rise2"), sb("w1_codes1", [P, N - P], U32, tag="rise3")]
+        w1_sc = [sb("w1_sc0", [P, P], U8), sb("w1_sc1", [P, N - P], U8)]
         z_codes = sb("z_codes", [P, H], U32)
         z_sc = sb("z_sc", [P, H], U8)
 
-        def quantize_w1(cols):
-            quantize(w1_codes[:, cols], w1_sc[:, cols], w1_bf[:, PACK * cols.start : PACK * cols.stop])
-
-        quantize_w1(slice(0, P))
+        quantize(w1_codes[0][:], w1_sc[0][:], w1_bf[:, 0 : PACK * P])
         for u in range(2):
             quantize(z_codes[:, HALVES[u]], z_sc[:, HALVES[u]], z_bf[u][:].rearrange("p c j -> p (c j)"))
-        quantize_w1(slice(P, 2 * P))
-        quantize_w1(slice(2 * P, 4 * P))
+        quantize(w1_codes[1][:, 0:P], w1_sc[1][:, 0:P], w1_bf[:, PACK * P : 2 * PACK * P])
+        quantize(w1_codes[1][:, P : 3 * P], w1_sc[1][:, P : 3 * P], w1_bf[:, 2 * PACK * P : 4 * PACK * P])
 
         h2 = [sb("h2_%d" % t, [P, H], F32) for t in range(PACK)]
         other = [sb("other%d" % t, [P, H], F32) for t in range(PACK)]
@@ -147,12 +154,12 @@ def tile_picked_tokfillhopp_none_p_kernel(tc, x_words, x_scales, wa, gt, w1, off
             if t == 0:
                 halves = [bank("h0_%d" % u, 5 + u, HALF)[:] for u in range(2)]
                 for u in range(2):
-                    product(halves[u], w1_codes, w1_sc, t, z_codes, z_sc, HALVES[u])
+                    product(halves[u], w1_codes[0], w1_sc[0], 0, z_codes, z_sc, HALVES[u])
                     nc.scalar.mul(h2[t][:, HALVES[u]], halves[u], 2.0)
             else:
                 acc = bank("h%d_acc" % t, (6 + t) % 8, H)
                 halves = [acc[:, HALVES[u]] for u in range(2)]
-                product(acc[:], w1_codes, w1_sc, t, z_codes, z_sc, slice(0, H))
+                product(acc[:], w1_codes[1], w1_sc[1], t - 1, z_codes, z_sc, slice(0, H))
                 nc.scalar.mul(h2[t][:], acc[:], 2.0)
                 if t in (1, 2):
                     nc.scalar.mul(other[t][:], acc[:], 2.0)
@@ -171,9 +178,9 @@ def tile_picked_tokfillhopp_none_p_kernel(tc, x_words, x_scales, wa, gt, w1, off
         for t in range(PACK):
             sig = sb("sig%d" % t, [P, H], F32)
             res = sb("res%d" % t, [P, H], F32)
-            for u in range(2):
-                nc.scalar.activation(sig[:, HALVES[u]], st2[t][:].indirect(n4_sb[:, LIST_HALVES[u]]), ACT.Sigmoid)
-            pieces = HALVES if t == PACK - 1 else (slice(0, H),)
+            pieces = (slice(0, 256), slice(256, 384), slice(384, 512)) if t == PACK - 1 else HALVES
             for cols in pieces:
+                nc.scalar.activation(sig[:, cols], st2[t][:].indirect(n4_sb[:, cols.start // 16 : cols.stop // 16]), ACT.Sigmoid)
+            for cols in pieces if t == PACK - 1 else (slice(0, H),):
                 nc.vector.scalar_tensor_tensor(res[:, cols], sig[:, cols], midpoint[:], st2[t][:, cols], ALU.subtract, ALU.mult)
                 nc.sync.dma_start(out_rows[:, t, cols], res[:, cols])

@@ -39,26 +39,40 @@ def tile_picked_tokfillhopp_none_p_kernel(tc, x_words, x_scales, wa, gt, w1, off
             nc.sync.dma_start(t[:], src)
             return t
 
-        all_scales = sb("all_scales", [P, T], U8)
-        nc.vector.memset(all_scales[:].bitcast(I32), 0)
+        scale_rows = sb("scale_rows", [P, T // 4], I32)
         for q in range(4):
-            nc.scalar.dma_start(all_scales[32 * q : 32 * q + 4, :].bitcast(I32), x_scales[0, 4 * q : 4 * q + 4, :].bitcast(I32))
+            nc.sync.dma_start(scale_rows[32 * q : 32 * q + 4, :], x_scales[0, 4 * q : 4 * q + 4, :].bitcast(I32))
+        wa_rows = wa.rearrange("(p j) c -> p j c", j=PACK)
+        wa_raw = [sb("wa_raw%d" % u, [P, PACK, HALF], F32) for u in range(2)]
+        nc.sync.dma_start(wa_raw[0][:], wa_rows[:, :, HALVES[0]])
+        offs_sb = load_list("offs_sb", offs)
+        nc.sync.dma_start(wa_raw[1][:], wa_rows[:, :, HALVES[1]])
+        all_words = sb("all_words", [P, T], I32)
+        nc.sync.dma_start(all_words[:], x_words[0].rearrange("p n r -> p (n r)").bitcast(I32))
+        n1_sb = load_list("n1_sb", n1)
+        n2_sb = load_list("n2_sb", n2)
+        w1_raw = sb("w1_raw", [P, PACK, N], F32)
+        gt_sb = sb("gt_sb", [P, PACK], F32)
+        for e in range(4):
+            nc.sync.dma_start(w1_raw[e:P:4, :, :], w1.rearrange("(a t e) m -> e a t m", t=PACK, e=4)[e])
+        with nc.allow_non_contiguous_dma(reason="gate weights, one value a token"):
+            for e in range(4):
+                nc.sync.dma_start(gt_sb[e:P:4, :], gt[:, 0].rearrange("(a t e) -> e a t", t=PACK, e=4)[e])
+        n3_sb = load_list("n3_sb", n3)
+        n4_sb = load_list("n4_sb", n4)
+
         zero = sb("zero", [P, 1], F32)
         nc.vector.memset(zero[:], 0.0)
         midpoint = sb("midpoint", [P, 1], F32)
         nc.scalar.activation(midpoint[:], zero[:], ACT.Sigmoid)
-
-        offs_sb = load_list("offs_sb", offs)
-        n1_sb = load_list("n1_sb", n1)
-        n2_sb = load_list("n2_sb", n2)
-        n3_sb = load_list("n3_sb", n3)
-        wa_rows = wa.rearrange("(p j) c -> p j c", j=PACK)
-        wa_raw = [sb("wa_raw%d" % u, [P, PACK, HALF], F32) for u in range(2)]
-        for u in range(2):
-            nc.sync.dma_start(wa_raw[u][:], wa_rows[:, :, HALVES[u]])
-        all_words = sb("all_words", [P, T], I32)
-        nc.sync.dma_start(all_words[:], x_words[0].rearrange("p n r -> p (n r)").bitcast(I32))
-        n4_sb = load_list("n4_sb", n4)
+        all_scales = sb("all_scales", [P, T], U8)
+        nc.vector.memset(all_scales[:].bitcast(I32), 0)
+        for q in range(4):
+            nc.vector.tensor_copy(all_scales[32 * q : 32 * q + 4, :].bitcast(I32), scale_rows[32 * q : 32 * q + 4, :])
+        picked_scales = sb("picked_scales", [P, S], U8)
+        nc.vector.tensor_copy(picked_scales[:], all_scales[:].indirect(offs_sb[:]))
+        x_sc = sb("x_sc", [P, S], U8)
+        nc.vector.tensor_copy(x_sc[:].bitcast(I32).rearrange("p (t a) -> p a t", t=PACK), picked_scales[:].bitcast(I32).rearrange("p (a t) -> p a t", t=PACK))
 
         wa_codes = sb("wa_codes", [P, H], U32)
         wa_sc = sb("wa_sc", [P, H], U8)
@@ -76,25 +90,13 @@ def tile_picked_tokfillhopp_none_p_kernel(tc, x_words, x_scales, wa, gt, w1, off
 
         for u in range(2):
             if u == 0:
-                cast_wa(nc.vector.tensor_copy, u, slice(0, HALF))
+                cast_wa(nc.scalar.copy, u, slice(0, HALF))
             else:
-                cast_wa(nc.vector.tensor_copy, u, slice(0, 160))
-                cast_wa(nc.scalar.copy, u, slice(160, HALF))
+                cast_wa(nc.vector.tensor_copy, u, slice(0, 192))
+                cast_wa(nc.scalar.copy, u, slice(192, HALF))
             quantize(wa_codes[:, HALVES[u]], wa_sc[:, HALVES[u]], wa_bf[u][:].rearrange("p c j -> p (c j)"))
 
-        w1_raw = sb("w1_raw", [P, PACK, N], F32, tag="wa_raw0")
-        gt_sb = sb("gt_sb", [P, PACK], F32, tag="wa_raw1")
-        for e in range(4):
-            nc.sync.dma_start(w1_raw[e:P:4, :, :], w1.rearrange("(a t e) m -> e a t m", t=PACK, e=4)[e])
-        with nc.allow_non_contiguous_dma(reason="gate weights, one value a token"):
-            for e in range(4):
-                nc.sync.dma_start(gt_sb[e:P:4, :], gt[:, 0].rearrange("(a t e) -> e a t", t=PACK, e=4)[e])
-
-        picked_scales = sb("picked_scales", [P, S], U8)
-        nc.vector.tensor_copy(picked_scales[:], all_scales[:].indirect(offs_sb[:]))
-        x_sc = sb("x_sc", [P, S], U8)
-        nc.vector.tensor_copy(x_sc[:].bitcast(I32).rearrange("p (t a) -> p a t", t=PACK), picked_scales[:].bitcast(I32).rearrange("p (a t) -> p a t", t=PACK))
-        x_codes = sb("x_codes", [P, S], U32, tag="picked_scales")
+        x_codes = sb("x_codes", [P, S], U32)
         nc.vector.tensor_copy(x_codes[:].rearrange("p (t a e) -> p a t e", t=PACK, e=4), all_words[:].bitcast(U32).indirect(offs_sb[:]))
 
         y = [sb("y%d" % t, [P, H], F32) for t in range(PACK)]
@@ -115,10 +117,10 @@ def tile_picked_tokfillhopp_none_p_kernel(tc, x_words, x_scales, wa, gt, w1, off
         for t in range(PACK):
             nc.vector.tensor_tensor(gap[:, W * t : W * (t + 1)], y[t][:].indirect(n2_sb[:]), pa[t][:], ALU.subtract)
 
-        w1_bf = sb("w1_bf", [P, N * PACK], BF16, tag="picked_scales")
+        w1_bf = sb("w1_bf", [P, N * PACK], BF16, tag="x_codes")
 
         def cast_w1(ms):
-            nc.scalar.copy(w1_bf[:].rearrange("p (t m j) -> p m t j", t=PACK, j=PACK)[:, ms], w1_raw[:].rearrange("p j (m t) -> p m t j", t=PACK)[:, ms])
+            nc.scalar.copy(w1_bf[:].rearrange("p (t m j) -> p m j t", t=PACK, j=PACK)[:, ms], w1_raw[:].rearrange("p j (m t) -> p m j t", t=PACK)[:, ms])
 
         for ms, tiles in ((slice(0, 96), (0, 1)), (slice(96, P), (2, 3))):
             cast_w1(ms)

@@ -16,10 +16,14 @@ ALU = mybir.AluOpType
 ACT = mybir.ActivationFunctionType
 
 P = 128
-PACK = 4
-HALF = H // 2
-HALVES = (slice(0, HALF), slice(HALF, H))
-LIST_HALVES = (slice(0, HALF // 16), slice(HALF // 16, H // 16))
+SLOTS = 4
+RUN = 4
+STRIPE = 16
+LAST = SLOTS - 1
+HALVES = (slice(0, H // 2), slice(H // 2, H))
+LAST_PIECES = (slice(0, H // 2), slice(H // 2, 3 * H // 4), slice(3 * H // 4, H))
+W1_GROUPS_FIRST = 96
+SUM_FROM_PSUM = ((0, 0), (0, 1), (LAST, 1))
 
 
 def tile_picked_tokfillhopp_none_p_kernel(tc, x_words, x_scales, wa, gt, w1, offs, n1, n2, n3, n4, out):
@@ -28,161 +32,177 @@ def tile_picked_tokfillhopp_none_p_kernel(tc, x_words, x_scales, wa, gt, w1, off
         keep = ctx.enter_context(tc.tile_pool(name="keep", bufs=1))
         psum = ctx.enter_context(tc.psum_pool(name="psum", bufs=1))
 
-        def sb(name, shape, dtype, tag=None):
-            return keep.tile(shape, dtype, name=name, tag=tag or name, align_bytes=64)
-
-        def bank(name, number, width):
-            return psum.tile([P, width], F32, name=name, tag="bank%d" % number)
+        def sbuf(name, shape, dtype, after=None):
+            return keep.tile(shape, dtype, name=name, tag=after or name, align_bytes=64)
 
         def load_list(name, src):
-            t = sb(name, list(src.shape), U16)
-            nc.sync.dma_start(t[:], src)
-            return t
+            entries = sbuf(name, list(src.shape), U16)
+            nc.sync.dma_start(entries[:], src)
+            return entries
 
-        scale_rows = sb("scale_rows", [P, T // 4], I32)
-        for q in range(4):
-            nc.sync.dma_start(scale_rows[32 * q : 32 * q + 4, :], x_scales[0, 4 * q : 4 * q + 4, :].bitcast(I32))
-        wa_rows = wa.rearrange("(p j) c -> p j c", j=PACK)
-        wa_raw = [sb("wa_raw%d" % u, [P, PACK, HALF], F32) for u in range(2)]
-        nc.sync.dma_start(wa_raw[0][:], wa_rows[:, :, HALVES[0]])
-        offs_sb = load_list("offs_sb", offs)
-        nc.sync.dma_start(wa_raw[1][:], wa_rows[:, :, HALVES[1]])
-        all_words = sb("all_words", [P, T], I32)
-        nc.sync.dma_start(all_words[:], x_words[0].rearrange("p n r -> p (n r)").bitcast(I32))
-        n1_sb = load_list("n1_sb", n1)
-        n2_sb = load_list("n2_sb", n2)
-        w1_raw = sb("w1_raw", [P, PACK, N], F32)
-        gt_sb = sb("gt_sb", [P, PACK], F32)
-        for e in range(4):
-            nc.sync.dma_start(w1_raw[e:P:4, :, :], w1.rearrange("(a t e) m -> e a t m", t=PACK, e=4)[e])
-        with nc.allow_non_contiguous_dma(reason="gate weights, one value a token"):
-            for e in range(4):
-                nc.sync.dma_start(gt_sb[e:P:4, :], gt[:, 0].rearrange("(a t e) -> e a t", t=PACK, e=4)[e])
-        n3_sb = load_list("n3_sb", n3)
-        n4_sb = load_list("n4_sb", n4)
-
-        zero = sb("zero", [P, 1], F32)
-        nc.vector.memset(zero[:], 0.0)
-        midpoint = sb("midpoint", [P, 1], F32)
-        nc.scalar.activation(midpoint[:], zero[:], ACT.Sigmoid)
-        all_scales = sb("all_scales", [P, T], U8)
-        nc.vector.memset(all_scales[:].bitcast(I32), 0)
-        for q in range(4):
-            nc.vector.tensor_copy(all_scales[32 * q : 32 * q + 4, :].bitcast(I32), scale_rows[32 * q : 32 * q + 4, :])
-        picked_scales = sb("picked_scales", [P, S], U8)
-        nc.vector.tensor_copy(picked_scales[:], all_scales[:].indirect(offs_sb[:]))
-        x_sc = sb("x_sc", [P, S], U8)
-        nc.vector.tensor_copy(x_sc[:].bitcast(I32).rearrange("p (t a) -> p a t", t=PACK), picked_scales[:].bitcast(I32).rearrange("p (a t) -> p a t", t=PACK))
-
-        wa_codes = sb("wa_codes", [P, H], U32)
-        wa_sc = sb("wa_sc", [P, H], U8)
-        wa_bf = [sb("wa_bf%d" % u, [P, HALF, PACK], BF16) for u in range(2)]
-
-        def cast_wa(copy, u, cols):
-            copy(wa_bf[u][:, cols, :].rearrange("p (c i) j -> p c j i", i=4), wa_raw[u][:, :, cols].rearrange("p j (c i) -> p c j i", i=4))
+        def list_part(entries, cols):
+            return entries[:, cols.start // STRIPE : cols.stop // STRIPE]
 
         def quantize(codes, scales, src):
             nc.vector.quantize_mx(out=codes.bitcast(FP8X4), scales=scales, in_=src)
 
-        def product(dst, l_codes, l_sc, t, r_codes, r_sc, cols):
-            rows = slice(P * t, P * (t + 1))
-            nc.tensor.matmul_mx(out=dst, lhsT=l_codes[:, rows].bitcast(FP8X4), lhsT_scale=l_sc[:, rows], rhs=r_codes[:, cols].bitcast(FP8X4), rhs_scale=r_sc[:, cols], start=True, stop=True)
+        def product(t, u, lhs_codes, lhs_scales, rhs_codes, rhs_scales):
+            acc = psum.tile([P, H // 2], F32, name="acc", tag="bank%d_%d" % (t, u))
+            nc.tensor.matmul_mx(
+                out=acc[:],
+                lhsT=lhs_codes.bitcast(FP8X4),
+                lhsT_scale=lhs_scales,
+                rhs=rhs_codes[:, HALVES[u]].bitcast(FP8X4),
+                rhs_scale=rhs_scales[:, HALVES[u]],
+                start=True,
+                stop=True,
+            )
+            return acc
 
+        scale_rows = sbuf("scale_rows", [P, T // 4], I32)
+        for q in range(4):
+            nc.sync.dma_start(scale_rows[32 * q : 32 * q + 4, :], x_scales[0, 4 * q : 4 * q + 4, :].bitcast(I32))
+        offs_sb = load_list("offs_sb", offs)
+        wa_raw = sbuf("wa_raw", [P, SLOTS, H], F32)
+        nc.sync.dma_start(wa_raw[:], wa.rearrange("(p j) c -> p j c", j=SLOTS))
+        all_words = sbuf("all_words", [P, T], I32)
+        nc.sync.dma_start(all_words[:], x_words[0].rearrange("p n r -> p (n r)").bitcast(I32))
+        n1_sb = load_list("n1_sb", n1)
+        n2_sb = load_list("n2_sb", n2)
+        w1_raw = sbuf("w1_raw", [P, SLOTS, N], F32)
+        gt_sb = sbuf("gt_sb", [P, SLOTS], F32)
+        for e in range(RUN):
+            nc.sync.dma_start(w1_raw[e:P:RUN, :, :], w1.rearrange("(a t e) m -> e a t m", t=SLOTS, e=RUN)[e])
+        with nc.allow_non_contiguous_dma(reason="gate weights, one value a token"):
+            for e in range(RUN):
+                nc.sync.dma_start(gt_sb[e:P:RUN, :], gt[:, 0].rearrange("(a t e) -> e a t", t=SLOTS, e=RUN)[e])
+        n3_sb = load_list("n3_sb", n3)
+        n4_sb = load_list("n4_sb", n4)
+
+        zero = sbuf("zero", [P, 1], F32)
+        nc.vector.memset(zero[:], 0.0)
+        midpoint = sbuf("midpoint", [P, 1], F32)
+        nc.scalar.activation(midpoint[:], zero[:], ACT.Sigmoid)
+
+        all_scales = sbuf("all_scales", [P, T], U8)
+        nc.vector.memset(all_scales[:].bitcast(I32), 0)
+        for q in range(4):
+            nc.vector.tensor_copy(all_scales[32 * q : 32 * q + 4, :].bitcast(I32), scale_rows[32 * q : 32 * q + 4, :])
+        picked_scales = sbuf("picked_scales", [P, S], U8)
+        nc.vector.tensor_copy(picked_scales[:], all_scales[:].indirect(offs_sb[:]))
+        x_sc = sbuf("x_sc", [P, S], U8)
+        nc.vector.tensor_copy(
+            x_sc[:].bitcast(I32).rearrange("p (t a) -> p a t", t=SLOTS),
+            picked_scales[:].bitcast(I32).rearrange("p (a t) -> p a t", t=SLOTS),
+        )
+
+        wa_codes = sbuf("wa_codes", [P, H], U32)
+        wa_sc = sbuf("wa_sc", [P, H], U8)
+        wa_bf = [sbuf("wa_bf%d" % u, [P, H // 2, SLOTS], BF16) for u in range(2)]
+        for u, copy in enumerate((nc.vector.tensor_copy, nc.scalar.copy)):
+            copy(
+                wa_bf[u][:].rearrange("p (c i) j -> p c j i", i=RUN),
+                wa_raw[:, :, HALVES[u]].rearrange("p j (c i) -> p c j i", i=RUN),
+            )
         for u in range(2):
-            if u == 0:
-                cast_wa(nc.scalar.copy, u, slice(0, HALF))
-            else:
-                cast_wa(nc.vector.tensor_copy, u, slice(0, 192))
-                cast_wa(nc.scalar.copy, u, slice(192, HALF))
             quantize(wa_codes[:, HALVES[u]], wa_sc[:, HALVES[u]], wa_bf[u][:].rearrange("p c j -> p (c j)"))
 
-        x_codes = sb("x_codes", [P, S], U32)
-        nc.vector.tensor_copy(x_codes[:].rearrange("p (t a e) -> p a t e", t=PACK, e=4), all_words[:].bitcast(U32).indirect(offs_sb[:]))
+        x_codes = sbuf("x_codes", [P, S], U32)
+        nc.vector.tensor_copy(
+            x_codes[:].rearrange("p (t a e) -> p a t e", t=SLOTS, e=RUN),
+            all_words[:].bitcast(U32).indirect(offs_sb[:]),
+        )
 
-        y = [sb("y%d" % t, [P, H], F32) for t in range(PACK)]
-        for u in range(2):
-            acc = bank("y0_%d" % u, u, HALF)
-            product(acc[:], x_codes, x_sc, 0, wa_codes, wa_sc, HALVES[u])
-            nc.scalar.copy(y[0][:, HALVES[u]], acc[:])
-        for t in range(1, PACK):
-            acc = bank("y%d_acc" % t, t + 1, H)
-            product(acc[:], x_codes, x_sc, t, wa_codes, wa_sc, slice(0, H))
-            nc.scalar.copy(y[t][:], acc[:])
+        y = [sbuf("y%d" % t, [P, H], F32) for t in range(SLOTS)]
+        for t in range(SLOTS):
+            tokens = slice(P * t, P * (t + 1))
+            for u in range(2):
+                acc = product(t, u, x_codes[:, tokens], x_sc[:, tokens], wa_codes, wa_sc)
+                copy = nc.vector.tensor_copy if (t, u) == (0, 0) else nc.scalar.copy
+                copy(y[t][:, HALVES[u]], acc[:])
 
-        pa = [sb("pa%d" % t, [P, W], F32) for t in range(PACK)]
-        gap = sb("gap", [P, PACK * W], F32, tag="wa_codes")
-        rise = [sb("rise%d" % t, [P, W], F32) for t in range(PACK)]
-        for t in range(PACK):
+        pa = [sbuf("pa%d" % t, [P, W], F32) for t in range(SLOTS)]
+        gap = sbuf("gap", [P, SLOTS * W], F32, after="wa_codes")
+        rise = [sbuf("rise%d" % t, [P, W], F32) for t in range(SLOTS)]
+        for t in range(SLOTS):
             nc.vector.tensor_copy(pa[t][:], y[t][:].indirect(n1_sb[:]))
-        for t in range(PACK):
+        for t in range(SLOTS):
             nc.vector.tensor_tensor(gap[:, W * t : W * (t + 1)], y[t][:].indirect(n2_sb[:]), pa[t][:], ALU.subtract)
 
-        w1_bf = sb("w1_bf", [P, N * PACK], BF16, tag="x_codes")
-
-        def cast_w1(ms):
-            nc.scalar.copy(w1_bf[:].rearrange("p (t m j) -> p m j t", t=PACK, j=PACK)[:, ms], w1_raw[:].rearrange("p j (m t) -> p m j t", t=PACK)[:, ms])
-
-        for ms, tiles in ((slice(0, 96), (0, 1)), (slice(96, P), (2, 3))):
-            cast_w1(ms)
+        w1_bf = sbuf("w1_bf", [P, N * SLOTS], BF16, after="x_codes")
+        for groups, tiles in ((slice(0, W1_GROUPS_FIRST), (0, 1)), (slice(W1_GROUPS_FIRST, P), (2, 3))):
+            nc.scalar.copy(
+                w1_bf[:].rearrange("p (t g j) -> p g j t", t=SLOTS, j=SLOTS)[:, groups],
+                w1_raw[:].rearrange("p j (g t) -> p g j t", t=SLOTS)[:, groups],
+            )
             for t in tiles:
                 nc.scalar.activation(rise[t][:], gap[:, W * t : W * (t + 1)], ACT.Relu)
-        z_bf = [sb("z_bf%d" % u, [P, HALF, PACK], BF16) for u in range(2)]
-        for t in range(PACK):
+
+        z_bf = [sbuf("z_bf%d" % u, [P, H // 2, SLOTS], BF16) for u in range(2)]
+        for t in range(SLOTS):
+            gate = gt_sb[:, t : t + 1]
             nc.vector.tensor_tensor(y[t][:].indirect(n1_sb[:]), pa[t][:], rise[t][:], ALU.add)
-            for u in range(2):
-                if t == PACK - 1 and u == 0:
-                    nc.vector.tensor_scalar(z_bf[u][:, :, t], y[t][:, HALVES[u]], gt_sb[:, t : t + 1], None, ALU.mult)
-                elif t == PACK - 2 and u == 0:
-                    nc.scalar.activation(z_bf[u][:, :, t : t + 2], y[t][:].rearrange("p (u c) -> p c u", u=2), ACT.Copy, scale=gt_sb[:, t : t + 1])
-                else:
-                    nc.scalar.activation(z_bf[u][:, :, t], y[t][:, HALVES[u]], ACT.Copy, scale=gt_sb[:, t : t + 1])
+            if t == LAST:
+                nc.vector.tensor_scalar(z_bf[0][:, :, t], y[t][:, HALVES[0]], gate, None, ALU.mult)
+            elif t == LAST - 1:
+                both_halves = y[t][:].rearrange("p (u c) -> p c u", u=2)
+                nc.scalar.activation(z_bf[0][:, :, t : t + 2], both_halves, ACT.Copy, scale=gate)
+            else:
+                nc.scalar.activation(z_bf[0][:, :, t], y[t][:, HALVES[0]], ACT.Copy, scale=gate)
+            nc.scalar.activation(z_bf[1][:, :, t], y[t][:, HALVES[1]], ACT.Copy, scale=gate)
 
-        w1_codes = [sb("w1_codes0", [P, P], U32, tag="rise2"), sb("w1_codes1", [P, N - P], U32, tag="rise3")]
-        w1_sc = [sb("w1_sc0", [P, P], U8), sb("w1_sc1", [P, N - P], U8)]
-        z_codes = sb("z_codes", [P, H], U32)
-        z_sc = sb("z_sc", [P, H], U8)
+        z_codes = sbuf("z_codes", [P, H], U32)
+        z_sc = sbuf("z_sc", [P, H], U8)
+        w1_operand = {}
 
-        quantize(w1_codes[0][:], w1_sc[0][:], w1_bf[:, 0 : PACK * P])
+        def quantize_w1(tiles, after):
+            width = P * len(tiles)
+            codes = sbuf("w1_codes%d" % tiles[0], [P, width], U32, after=after)
+            scales = sbuf("w1_sc%d" % tiles[0], [P, width], U8)
+            first = SLOTS * P * tiles[0]
+            quantize(codes[:], scales[:], w1_bf[:, first : first + SLOTS * width])
+            for place, t in enumerate(tiles):
+                places = slice(P * place, P * (place + 1))
+                w1_operand[t] = (codes[:, places], scales[:, places])
+
+        quantize_w1((0,), "rise2")
         for u in range(2):
             quantize(z_codes[:, HALVES[u]], z_sc[:, HALVES[u]], z_bf[u][:].rearrange("p c j -> p (c j)"))
-        quantize(w1_codes[1][:, 0:P], w1_sc[1][:, 0:P], w1_bf[:, PACK * P : 2 * PACK * P])
-        quantize(w1_codes[1][:, P : 3 * P], w1_sc[1][:, P : 3 * P], w1_bf[:, 2 * PACK * P : 4 * PACK * P])
+        quantize_w1((1,), "rise3")
+        quantize_w1((2, 3), "z_bf1")
 
-        h2 = [sb("h2_%d" % t, [P, H], F32) for t in range(PACK)]
-        other = [sb("other%d" % t, [P, H], F32) for t in range(PACK)]
-        st2 = [sb("st2_%d" % t, [P, H], F32) for t in range(PACK)]
-        accs = []
-        for t in range(PACK):
-            if t == 0:
-                halves = [bank("h0_%d" % u, 5 + u, HALF)[:] for u in range(2)]
-                for u in range(2):
-                    product(halves[u], w1_codes[0], w1_sc[0], 0, z_codes, z_sc, HALVES[u])
-                    nc.scalar.mul(h2[t][:, HALVES[u]], halves[u], 2.0)
-            else:
-                acc = bank("h%d_acc" % t, (6 + t) % 8, H)
-                halves = [acc[:, HALVES[u]] for u in range(2)]
-                product(acc[:], w1_codes[1], w1_sc[1], t - 1, z_codes, z_sc, slice(0, H))
-                nc.scalar.mul(h2[t][:], acc[:], 2.0)
-                if t in (1, 2):
-                    nc.scalar.mul(other[t][:], acc[:], 2.0)
-            accs.append(halves)
-        for t in range(PACK):
-            if t in (1, 2):
-                for u in range(2):
-                    nc.vector.tensor_tensor(st2[t][:, HALVES[u]], h2[t][:].indirect(n3_sb[:, LIST_HALVES[u]]), other[t][:, HALVES[u]], ALU.add)
-            else:
-                for u in range(2):
-                    nc.vector.tensor_copy(other[t][:, HALVES[u]], h2[t][:].indirect(n3_sb[:, LIST_HALVES[u]]))
-                for u in range(2):
-                    nc.vector.scalar_tensor_tensor(st2[t][:, HALVES[u]], accs[t][u], 2.0, other[t][:, HALVES[u]], ALU.mult, ALU.add)
+        h2 = [sbuf("h2_%d" % t, [P, H], F32) for t in range(SLOTS)]
+        addend = [sbuf("addend%d" % t, [P, H], F32) for t in range(SLOTS)]
+        st2 = [sbuf("st2_%d" % t, [P, H], F32) for t in range(SLOTS)]
+        h_acc = {}
+        for t in range(SLOTS):
+            for u in range(2):
+                h_acc[t, u] = product(t, u, w1_operand[t][0], w1_operand[t][1], z_codes, z_sc)
+                nc.scalar.mul(h2[t][:, HALVES[u]], h_acc[t, u][:], 2.0)
+            for u in range(2):
+                if (t, u) not in SUM_FROM_PSUM:
+                    nc.scalar.mul(addend[t][:, HALVES[u]], h_acc[t, u][:], 2.0)
+        for t in range(SLOTS):
+            for u in (1, 0):
+                looked_up = h2[t][:].indirect(list_part(n3_sb, HALVES[u]))
+                if (t, u) in SUM_FROM_PSUM:
+                    nc.vector.tensor_copy(addend[t][:, HALVES[u]], looked_up)
+                else:
+                    nc.vector.tensor_tensor(st2[t][:, HALVES[u]], looked_up, addend[t][:, HALVES[u]], ALU.add)
+            for u in (1, 0):
+                if (t, u) in SUM_FROM_PSUM:
+                    nc.vector.scalar_tensor_tensor(
+                        st2[t][:, HALVES[u]], h_acc[t, u][:], 2.0, addend[t][:, HALVES[u]], ALU.mult, ALU.add
+                    )
 
-        out_rows = out.rearrange("(p t) c -> p t c", t=PACK)
-        for t in range(PACK):
-            sig = sb("sig%d" % t, [P, H], F32)
-            res = sb("res%d" % t, [P, H], F32)
-            pieces = (slice(0, 256), slice(256, 384), slice(384, 512)) if t == PACK - 1 else HALVES
-            for cols in pieces:
-                nc.scalar.activation(sig[:, cols], st2[t][:].indirect(n4_sb[:, cols.start // 16 : cols.stop // 16]), ACT.Sigmoid)
-            for cols in pieces if t == PACK - 1 else (slice(0, H),):
-                nc.vector.scalar_tensor_tensor(res[:, cols], sig[:, cols], midpoint[:], st2[t][:, cols], ALU.subtract, ALU.mult)
-                nc.sync.dma_start(out_rows[:, t, cols], res[:, cols])
+        out_rows = out.rearrange("(p t) c -> p t c", t=SLOTS)
+        for t in range(SLOTS):
+            sig = sbuf("sig%d" % t, [P, H], F32)
+            result = sbuf("result%d" % t, [P, H], F32)
+            for cols in LAST_PIECES if t == LAST else HALVES:
+                nc.scalar.activation(sig[:, cols], st2[t][:].indirect(list_part(n4_sb, cols)), ACT.Sigmoid)
+            for cols in LAST_PIECES if t == LAST else (slice(0, H),):
+                nc.vector.scalar_tensor_tensor(
+                    result[:, cols], sig[:, cols], midpoint[:], st2[t][:, cols], ALU.subtract, ALU.mult
+                )
+                nc.sync.dma_start(out_rows[:, t, cols], result[:, cols])

@@ -23,7 +23,7 @@ LAST = SLOTS - 1
 HALVES = (slice(0, H // 2), slice(H // 2, H))
 LAST_PIECES = (slice(0, H // 2), slice(H // 2, 3 * H // 4), slice(3 * H // 4, H))
 W1_GROUPS_FIRST = 96
-SUM_FROM_PSUM = ((0, 0), (0, 1), (LAST, 1))
+SUM_FROM_PSUM = ((0, 0), (0, 1))
 
 
 def tile_picked_tokfillhopp_none_p_kernel(tc, x_words, x_scales, wa, gt, w1, offs, n1, n2, n3, n4, out):
@@ -144,12 +144,17 @@ def tile_picked_tokfillhopp_none_p_kernel(tc, x_words, x_scales, wa, gt, w1, off
             nc.vector.tensor_tensor(y[t][:].indirect(n1_sb[:]), pa[t][:], rise[t][:], ALU.add)
             if t == LAST:
                 nc.vector.tensor_scalar(z_bf[0][:, :, t], y[t][:, HALVES[0]], gate, None, ALU.mult)
+                nc.vector.tensor_scalar(z_bf[1][:, 0:P, t], y[t][:, 2 * P : 3 * P], gate, None, ALU.mult)
+                nc.scalar.activation(z_bf[1][:, P : 2 * P, t], y[t][:, 3 * P : 4 * P], ACT.Copy, scale=gate)
             elif t == LAST - 1:
                 both_halves = y[t][:].rearrange("p (u c) -> p c u", u=2)
                 nc.scalar.activation(z_bf[0][:, :, t : t + 2], both_halves, ACT.Copy, scale=gate)
+                last_quarters = y[t][:, HALVES[1]].rearrange("p (u c) -> p c u", u=2)
+                nc.scalar.activation(z_bf[1][:, 0:P, t : t + 2], last_quarters, ACT.Copy, scale=gate)
+                nc.scalar.activation(z_bf[1][:, P : 2 * P, t], y[t][:, 3 * P : 4 * P], ACT.Copy, scale=gate)
             else:
-                nc.scalar.activation(z_bf[0][:, :, t], y[t][:, HALVES[0]], ACT.Copy, scale=gate)
-            nc.scalar.activation(z_bf[1][:, :, t], y[t][:, HALVES[1]], ACT.Copy, scale=gate)
+                for u in range(2):
+                    nc.scalar.activation(z_bf[u][:, :, t], y[t][:, HALVES[u]], ACT.Copy, scale=gate)
 
         z_codes = sbuf("z_codes", [P, H], U32)
         z_sc = sbuf("z_sc", [P, H], U8)
@@ -180,8 +185,10 @@ def tile_picked_tokfillhopp_none_p_kernel(tc, x_words, x_scales, wa, gt, w1, off
                 h_acc[t, u] = product(t, u, w1_operand[t][0], w1_operand[t][1], z_codes, z_sc)
                 nc.scalar.mul(h2[t][:, HALVES[u]], h_acc[t, u][:], 2.0)
             for u in range(2):
-                if (t, u) not in SUM_FROM_PSUM:
+                if t == LAST:
                     nc.scalar.mul(addend[t][:, HALVES[u]], h_acc[t, u][:], 2.0)
+                elif t > 0:
+                    nc.gpsimd.tensor_scalar(addend[t][:, HALVES[u]], h2[t][:, HALVES[u]], 1.0, 0.0, ALU.mult, ALU.add)
         for t in range(SLOTS):
             for u in (1, 0):
                 looked_up = h2[t][:].indirect(list_part(n3_sb, HALVES[u]))

from contextlib import ExitStack

import concourse.mybir as mybir

K, T, S, N, H, W = 512, 2048, 512, 512, 512, 256
FLOPS = 2 * K * S * H + 2 * S * N * H

F32 = mybir.dt.float32
BF16 = mybir.dt.bfloat16
I32 = mybir.dt.int32
U32 = mybir.dt.uint32
U16 = mybir.dt.uint16
U8 = mybir.dt.uint8
FP8X4 = mybir.dt.float8_e4m3fn_x4
ALU = mybir.AluOpType
ACT = mybir.ActivationFunctionType

P = 128
SLOTS = 4
RUN = 4
STRIPE = 16
LAST = SLOTS - 1
HALVES = (slice(0, H // 2), slice(H // 2, H))
LAST_PIECES = (slice(0, H // 2), slice(H // 2, 3 * H // 4), slice(3 * H // 4, H))
W1_GROUPS_FIRST = 96
SUM_FROM_PSUM = ((0, 0), (0, 1))


def tile_picked_tokfillhopp_none_p_kernel(tc, x_words, x_scales, wa, gt, w1, offs, n1, n2, n3, n4, out):
    nc = tc.nc
    with ExitStack() as ctx:
        keep = ctx.enter_context(tc.tile_pool(name="keep", bufs=1))
        psum = ctx.enter_context(tc.psum_pool(name="psum", bufs=1))

        def sbuf(name, shape, dtype, after=None):
            return keep.tile(shape, dtype, name=name, tag=after or name, align_bytes=64)

        def load_list(name, src):
            entries = sbuf(name, list(src.shape), U16)
            nc.sync.dma_start(entries[:], src)
            return entries

        def list_part(entries, cols):
            return entries[:, cols.start // STRIPE : cols.stop // STRIPE]

        def quantize(codes, scales, src):
            nc.vector.quantize_mx(out=codes.bitcast(FP8X4), scales=scales, in_=src)

        def product(t, u, lhs_codes, lhs_scales, rhs_codes, rhs_scales):
            acc = psum.tile([P, H // 2], F32, name="acc", tag="bank%d_%d" % (t, u))
            nc.tensor.matmul_mx(
                out=acc[:],
                lhsT=lhs_codes.bitcast(FP8X4),
                lhsT_scale=lhs_scales,
                rhs=rhs_codes[:, HALVES[u]].bitcast(FP8X4),
                rhs_scale=rhs_scales[:, HALVES[u]],
                start=True,
                stop=True,
            )
            return acc

        scale_rows = sbuf("scale_rows", [P, T // 4], I32)
        for q in range(4):
            nc.sync.dma_start(scale_rows[32 * q : 32 * q + 4, :], x_scales[0, 4 * q : 4 * q + 4, :].bitcast(I32))
        offs_sb = load_list("offs_sb", offs)
        wa_raw = sbuf("wa_raw", [P, SLOTS, H], F32)
        nc.sync.dma_start(wa_raw[:], wa.rearrange("(p j) c -> p j c", j=SLOTS))
        all_words = sbuf("all_words", [P, T], I32)
        nc.sync.dma_start(all_words[:], x_words[0].rearrange("p n r -> p (n r)").bitcast(I32))
        n1_sb = load_list("n1_sb", n1)
        n2_sb = load_list("n2_sb", n2)
        w1_raw = sbuf("w1_raw", [P, SLOTS, N], F32)
        gt_sb = sbuf("gt_sb", [P, SLOTS], F32)
        for e in range(RUN):
            nc.sync.dma_start(w1_raw[e:P:RUN, :, :], w1.rearrange("(a t e) m -> e a t m", t=SLOTS, e=RUN)[e])
        with nc.allow_non_contiguous_dma(reason="gate weights, one value a token"):
            for e in range(RUN):
                nc.sync.dma_start(gt_sb[e:P:RUN, :], gt[:, 0].rearrange("(a t e) -> e a t", t=SLOTS, e=RUN)[e])
        n3_sb = load_list("n3_sb", n3)
        n4_sb = load_list("n4_sb", n4)

        zero = sbuf("zero", [P, 1], F32)
        nc.vector.memset(zero[:], 0.0)
        midpoint = sbuf("midpoint", [P, 1], F32)
        nc.scalar.activation(midpoint[:], zero[:], ACT.Sigmoid)

        all_scales = sbuf("all_scales", [P, T], U8)
        nc.vector.memset(all_scales[:].bitcast(I32), 0)
        for q in range(4):
            nc.vector.tensor_copy(all_scales[32 * q : 32 * q + 4, :].bitcast(I32), scale_rows[32 * q : 32 * q + 4, :])
        picked_scales = sbuf("picked_scales", [P, S], U8)
        nc.vector.tensor_copy(picked_scales[:], all_scales[:].indirect(offs_sb[:]))
        x_sc = sbuf("x_sc", [P, S], U8)
        nc.vector.tensor_copy(
            x_sc[:].bitcast(I32).rearrange("p (t a) -> p a t", t=SLOTS),
            picked_scales[:].bitcast(I32).rearrange("p (a t) -> p a t", t=SLOTS),
        )

        wa_codes = sbuf("wa_codes", [P, H], U32)
        wa_sc = sbuf("wa_sc", [P, H], U8)
        wa_bf = [sbuf("wa_bf%d" % u, [P, H // 2, SLOTS], BF16) for u in range(2)]
        for u, copy in enumerate((nc.vector.tensor_copy, nc.scalar.copy)):
            copy(
                wa_bf[u][:].rearrange("p (c i) j -> p c j i", i=RUN),
                wa_raw[:, :, HALVES[u]].rearrange("p j (c i) -> p c j i", i=RUN),
            )
        for u in range(2):
            quantize(wa_codes[:, HALVES[u]], wa_sc[:, HALVES[u]], wa_bf[u][:].rearrange("p c j -> p (c j)"))

        x_codes = sbuf("x_codes", [P, S], U32)
        nc.vector.tensor_copy(
            x_codes[:].rearrange("p (t a e) -> p a t e", t=SLOTS, e=RUN),
            all_words[:].bitcast(U32).indirect(offs_sb[:]),
        )

        y = [sbuf("y%d" % t, [P, H], F32) for t in range(SLOTS)]
        for t in range(SLOTS):
            tokens = slice(P * t, P * (t + 1))
            for u in range(2):
                acc = product(t, u, x_codes[:, tokens], x_sc[:, tokens], wa_codes, wa_sc)
                copy = nc.vector.tensor_copy if (t, u) == (0, 0) else nc.scalar.copy
                copy(y[t][:, HALVES[u]], acc[:])

        pa = [sbuf("pa%d" % t, [P, W], F32) for t in range(SLOTS)]
        gap = sbuf("gap", [P, SLOTS * W], F32, after="wa_codes")
        rise = [sbuf("rise%d" % t, [P, W], F32) for t in range(SLOTS)]
        for t in range(SLOTS):
            nc.vector.tensor_copy(pa[t][:], y[t][:].indirect(n1_sb[:]))
        for t in range(SLOTS):
            nc.vector.tensor_tensor(gap[:, W * t : W * (t + 1)], y[t][:].indirect(n2_sb[:]), pa[t][:], ALU.subtract)

        w1_bf = sbuf("w1_bf", [P, N * SLOTS], BF16, after="x_codes")
        for groups, tiles in ((slice(0, W1_GROUPS_FIRST), (0, 1)), (slice(W1_GROUPS_FIRST, P), (2, 3))):
            nc.scalar.copy(
                w1_bf[:].rearrange("p (t g j) -> p g j t", t=SLOTS, j=SLOTS)[:, groups],
                w1_raw[:].rearrange("p j (g t) -> p g j t", t=SLOTS)[:, groups],
            )
            for t in tiles:
                nc.scalar.activation(rise[t][:], gap[:, W * t : W * (t + 1)], ACT.Relu)

        z_bf = [sbuf("z_bf%d" % u, [P, H // 2, SLOTS], BF16) for u in range(2)]
        for t in range(SLOTS):
            gate = gt_sb[:, t : t + 1]
            nc.vector.tensor_tensor(y[t][:].indirect(n1_sb[:]), pa[t][:], rise[t][:], ALU.add)
            if t == LAST:
                nc.vector.tensor_scalar(z_bf[0][:, :, t], y[t][:, HALVES[0]], gate, None, ALU.mult)
                nc.vector.tensor_scalar(z_bf[1][:, 0:P, t], y[t][:, 2 * P : 3 * P], gate, None, ALU.mult)
                nc.scalar.activation(z_bf[1][:, P : 2 * P, t], y[t][:, 3 * P : 4 * P], ACT.Copy, scale=gate)
            elif t == LAST - 1:
                both_halves = y[t][:].rearrange("p (u c) -> p c u", u=2)
                nc.scalar.activation(z_bf[0][:, :, t : t + 2], both_halves, ACT.Copy, scale=gate)
                last_quarters = y[t][:, HALVES[1]].rearrange("p (u c) -> p c u", u=2)
                nc.scalar.activation(z_bf[1][:, 0:P, t : t + 2], last_quarters, ACT.Copy, scale=gate)
                nc.scalar.activation(z_bf[1][:, P : 2 * P, t], y[t][:, 3 * P : 4 * P], ACT.Copy, scale=gate)
            else:
                for u in range(2):
                    nc.scalar.activation(z_bf[u][:, :, t], y[t][:, HALVES[u]], ACT.Copy, scale=gate)

        z_codes = sbuf("z_codes", [P, H], U32)
        z_sc = sbuf("z_sc", [P, H], U8)
        w1_operand = {}

        def quantize_w1(tiles, after):
            width = P * len(tiles)
            codes = sbuf("w1_codes%d" % tiles[0], [P, width], U32, after=after)
            scales = sbuf("w1_sc%d" % tiles[0], [P, width], U8)
            first = SLOTS * P * tiles[0]
            quantize(codes[:], scales[:], w1_bf[:, first : first + SLOTS * width])
            for place, t in enumerate(tiles):
                places = slice(P * place, P * (place + 1))
                w1_operand[t] = (codes[:, places], scales[:, places])

        quantize_w1((0,), "rise2")
        for u in range(2):
            quantize(z_codes[:, HALVES[u]], z_sc[:, HALVES[u]], z_bf[u][:].rearrange("p c j -> p (c j)"))
        quantize_w1((1,), "rise3")
        quantize_w1((2, 3), "z_bf1")

        h2 = [sbuf("h2_%d" % t, [P, H], F32) for t in range(SLOTS)]
        addend = [sbuf("addend%d" % t, [P, H], F32) for t in range(SLOTS)]
        st2 = [sbuf("st2_%d" % t, [P, H], F32) for t in range(SLOTS)]
        h_acc = {}
        for t in range(SLOTS):
            for u in range(2):
                h_acc[t, u] = product(t, u, w1_operand[t][0], w1_operand[t][1], z_codes, z_sc)
                nc.scalar.mul(h2[t][:, HALVES[u]], h_acc[t, u][:], 2.0)
            for u in range(2):
                if t == LAST:
                    nc.scalar.mul(addend[t][:, HALVES[u]], h_acc[t, u][:], 2.0)
                elif t > 0:
                    nc.gpsimd.tensor_scalar(addend[t][:, HALVES[u]], h2[t][:, HALVES[u]], 1.0, 0.0, ALU.mult, ALU.add)
        for t in range(SLOTS):
            for u in (1, 0):
                looked_up = h2[t][:].indirect(list_part(n3_sb, HALVES[u]))
                if (t, u) in SUM_FROM_PSUM:
                    nc.vector.tensor_copy(addend[t][:, HALVES[u]], looked_up)
                else:
                    nc.vector.tensor_tensor(st2[t][:, HALVES[u]], looked_up, addend[t][:, HALVES[u]], ALU.add)
            for u in (1, 0):
                if (t, u) in SUM_FROM_PSUM:
                    nc.vector.scalar_tensor_tensor(
                        st2[t][:, HALVES[u]], h_acc[t, u][:], 2.0, addend[t][:, HALVES[u]], ALU.mult, ALU.add
                    )

        out_rows = out.rearrange("(p t) c -> p t c", t=SLOTS)
        for t in range(SLOTS):
            sig = sbuf("sig%d" % t, [P, H], F32)
            result = sbuf("result%d" % t, [P, H], F32)
            for cols in LAST_PIECES if t == LAST else HALVES:
                nc.scalar.activation(sig[:, cols], st2[t][:].indirect(list_part(n4_sb, cols)), ACT.Sigmoid)
            for cols in LAST_PIECES if t == LAST else (slice(0, H),):
                nc.vector.scalar_tensor_tensor(
                    result[:, cols], sig[:, cols], midpoint[:], st2[t][:, cols], ALU.subtract, ALU.mult
                )
                nc.sync.dma_start(out_rows[:, t, cols], result[:, cols])
